import numpy as np
import ml_dtypes

BF16 = ml_dtypes.bfloat16


def bf(x):
    return np.asarray(x, np.float32).astype(BF16)


def f32(x):
    return np.asarray(x, np.float32)


def f64(x):
    return np.asarray(x).astype(np.float64)


def striped(idx):
    return np.tile(idx.reshape(-1, 16).T, (8, 1))


S, K, M, N, E, Q, O = 512, 128, 256, 512, 2, 256, 512


def sigmoid(v):
    return 1.0 / (1.0 + np.exp(-v))


def setup_inputs():
    return {"base": bf(np.random.standard_normal((M, S))), "x": bf(np.random.standard_normal((K, N))), "w": bf(1.2 * np.random.standard_normal((E, K, M)) / np.sqrt(K)), "w2": bf(np.random.standard_normal((M, O)) / np.sqrt(2 * M)), "b": f32(0.5 * np.random.standard_normal((O, 1))), "offs": striped(np.random.permutation(S))}


def reference(base, x, w, w2, b, offs):
    idx = offs[:16].T.reshape(-1)
    z = f64(base).copy()
    for e in range(E):
        z[:, idx[e * Q : (e + 1) * Q]] += f64(w)[e].T @ f64(x)[:, e * Q : (e + 1) * Q]
    y = f64(w2).T @ z
    return (y + f64(b)) * sigmoid(y + f64(b))

@@ -1,0 +1,70 @@
+import concourse.mybir as mybir
+from concourse.masks import make_identity
+
+BF16, F32, U16 = mybir.dt.bfloat16, mybir.dt.float32, mybir.dt.uint16
+SILU = mybir.ActivationFunctionType.Silu
+
+P = 128
+S, K, M, N, E, Q, O = 512, 128, 256, 512, 2, 256, 512
+M_BLOCKS = M // P
+O_BLOCKS = O // P
+PIECE = Q // 16
+
+FLOPS = 2 * K * M * N + 2 * M * O * S
+
+
+def tile_rows_thenproj_silu_kernel(tc, base, x, w, w2, b, offs, out):
+    nc = tc.nc
+    with (
+        tc.tile_pool(name="held", bufs=1) as held,
+        tc.psum_pool(name="psum", bufs=1) as psum,
+    ):
+        base_sb = held.tile([P, M_BLOCKS, S], BF16)
+        x_sb = held.tile([P, N], BF16)
+        w_sb = held.tile([P, E, M], BF16)
+        offsets = held.tile([P, N // 16], U16)
+        w2_sb = held.tile([P, M_BLOCKS, O], BF16)
+        bias = held.tile([P, O_BLOCKS], F32)
+        nc.sync.dma_start(base_sb[:], base.rearrange("(a p) s -> p a s", p=P))
+        nc.sync.dma_start(x_sb[:], x)
+        nc.sync.dma_start(w_sb[:], w.rearrange("e k m -> k e m"))
+        nc.sync.dma_start(offsets[:], offs)
+        nc.sync.dma_start(w2_sb[:], w2.rearrange("(a p) o -> p a o", p=P))
+        nc.scalar.dma_start(bias[:], b.rearrange("(a p) t -> p (a t)", p=P))
+
+        ident = held.tile([P, P], BF16)
+        make_identity(nc, ident[:])
+
+        windows = [psum.tile([P, S], F32, name=f"window{a}") for a in range(M_BLOCKS)]
+        for a in range(M_BLOCKS):
+            nc.tensor.matmul(windows[a][:], ident[:], base_sb[:, a, :], start=True, stop=False)
+
+        for a in range(M_BLOCKS):
+            for e in range(E):
+                nc.tensor.matmul(
+                    windows[a][:].indirect(offsets[:, e * PIECE : (e + 1) * PIECE]),
+                    w_sb[:, e, a * P : (a + 1) * P],
+                    x_sb[:, e * Q : (e + 1) * Q],
+                    start=False,
+                    stop=(e == E - 1),
+                )
+
+        z_sb = held.tile([P, M_BLOCKS, S], BF16)
+        for a in range(M_BLOCKS):
+            nc.vector.tensor_copy(z_sb[:, a, :], windows[a][:])
+
+        y = [psum.tile([P, S], F32, name=f"y{o}") for o in range(O_BLOCKS)]
+        for a in range(M_BLOCKS):
+            for o in range(O_BLOCKS):
+                nc.tensor.matmul(
+                    y[o][:],
+                    w2_sb[:, a, o * P : (o + 1) * P],
+                    z_sb[:, a, :],
+                    start=(a == 0),
+                    stop=(a == M_BLOCKS - 1),
+                )
+
+        out_sb = held.tile([P, O_BLOCKS, S], F32)
+        for o in range(O_BLOCKS):
+            nc.scalar.activation(out_sb[:, o, :], y[o][:], SILU, bias=bias[:, o : o + 1])
+            nc.sync.dma_start(out[o * P : (o + 1) * P, :], out_sb[:, o, :])

@@ -10,6 +10,8 @@ M_BLOCKS = M // P
 O_BLOCKS = O // P
 PIECE = Q // 16
 
+WARM_UP = 4
+
 FLOPS = 2 * K * M * N + 2 * M * O * S
 
 
@@ -34,6 +36,14 @@ def tile_rows_thenproj_silu_kernel(tc, base, x, w, w2, b, offs, out):
 
         ident = held.tile([P, P], BF16)
         make_identity(nc, ident[:])
+
+        zeros = held.tile([P, S], BF16)
+        nc.vector.memset(zeros[:], 0.0)
+        idle_bank = psum.tile([P, S], F32)
+        for i in range(WARM_UP):
+            nc.tensor.matmul(idle_bank[:], zeros[:, :P], zeros[:], start=True, stop=True)
+        silu_of_zero = held.tile([P, 1], F32)
+        nc.scalar.activation(silu_of_zero[:], zeros[:, 0:1], SILU)
 
         windows = [psum.tile([P, S], F32, name=f"window{a}") for a in range(M_BLOCKS)]
         for a in range(M_BLOCKS):

@@ -8,6 +8,8 @@ P = 128
 S, K, M, N, E, Q, O = 512, 128, 256, 512, 2, 256, 512
 M_BLOCKS = M // P
 O_BLOCKS = O // P
+H = 2
+HALF = S // H
 PIECE = Q // 16
 
 WARM_UP = 4
@@ -61,20 +63,23 @@ def tile_rows_thenproj_silu_kernel(tc, base, x, w, w2, b, offs, out):
 
         z_sb = held.tile([P, M_BLOCKS, S], BF16)
         for a in range(M_BLOCKS):
-            nc.vector.tensor_copy(z_sb[:, a, :], windows[a][:])
+            for h in range(H):
+                cols = slice(h * HALF, (h + 1) * HALF)
+                nc.vector.tensor_copy(z_sb[:, a, cols], windows[a][:, cols])
 
         y = [psum.tile([P, S], F32, name=f"y{o}") for o in range(O_BLOCKS)]
-        for a in range(M_BLOCKS):
-            for o in range(O_BLOCKS):
-                nc.tensor.matmul(
-                    y[o][:],
-                    w2_sb[:, a, o * P : (o + 1) * P],
-                    z_sb[:, a, :],
-                    start=(a == 0),
-                    stop=(a == M_BLOCKS - 1),
-                )
-
         out_sb = held.tile([P, O_BLOCKS, S], F32)
-        for o in range(O_BLOCKS):
-            nc.scalar.activation(out_sb[:, o, :], y[o][:], SILU, bias=bias[:, o : o + 1])
-            nc.sync.dma_start(out[o * P : (o + 1) * P, :], out_sb[:, o, :])
+        for h in range(H):
+            cols = slice(h * HALF, (h + 1) * HALF)
+            for a in range(M_BLOCKS):
+                for o in range(O_BLOCKS):
+                    nc.tensor.matmul(
+                        y[o][:, cols],
+                        w2_sb[:, a, o * P : (o + 1) * P],
+                        z_sb[:, a, cols],
+                        start=(a == 0),
+                        stop=(a == M_BLOCKS - 1),
+                    )
+            for o in range(O_BLOCKS):
+                nc.scalar.activation(out_sb[:, o, cols], y[o][:, cols], SILU, bias=bias[:, o : o + 1])
+                nc.sync.dma_start(out[o * P : (o + 1) * P, cols], out_sb[:, o, cols])

@@ -12,7 +12,7 @@ H = 2
 HALF = S // H
 PIECE = Q // 16
 
-WARM_UP = 4
+WARM_UP = 3
 
 FLOPS = 2 * K * M * N + 2 * M * O * S
 

@@ -34,7 +34,7 @@ def tile_rows_thenproj_silu_kernel(tc, base, x, w, w2, b, offs, out):
         nc.sync.dma_start(w_sb[:], w.rearrange("e k m -> k e m"))
         nc.sync.dma_start(offsets[:], offs)
         nc.sync.dma_start(w2_sb[:], w2.rearrange("(a p) o -> p a o", p=P))
-        nc.scalar.dma_start(bias[:], b.rearrange("(a p) t -> p (a t)", p=P))
+        nc.sync.dma_start(bias[:], b.rearrange("(a p) t -> p (a t)", p=P))
 
         ident = held.tile([P, P], BF16)
         make_identity(nc, ident[:])

import concourse.mybir as mybir
from concourse.masks import make_identity

BF16, F32, U16 = mybir.dt.bfloat16, mybir.dt.float32, mybir.dt.uint16
SILU = mybir.ActivationFunctionType.Silu

P = 128
S, K, M, N, E, Q, O = 512, 128, 256, 512, 2, 256, 512
M_BLOCKS = M // P
O_BLOCKS = O // P
H = 2
HALF = S // H
PIECE = Q // 16

WARM_UP = 3

FLOPS = 2 * K * M * N + 2 * M * O * S


def tile_rows_thenproj_silu_kernel(tc, base, x, w, w2, b, offs, out):
    nc = tc.nc
    with (
        tc.tile_pool(name="held", bufs=1) as held,
        tc.psum_pool(name="psum", bufs=1) as psum,
    ):
        base_sb = held.tile([P, M_BLOCKS, S], BF16)
        x_sb = held.tile([P, N], BF16)
        w_sb = held.tile([P, E, M], BF16)
        offsets = held.tile([P, N // 16], U16)
        w2_sb = held.tile([P, M_BLOCKS, O], BF16)
        bias = held.tile([P, O_BLOCKS], F32)
        nc.sync.dma_start(base_sb[:], base.rearrange("(a p) s -> p a s", p=P))
        nc.sync.dma_start(x_sb[:], x)
        nc.sync.dma_start(w_sb[:], w.rearrange("e k m -> k e m"))
        nc.sync.dma_start(offsets[:], offs)
        nc.sync.dma_start(w2_sb[:], w2.rearrange("(a p) o -> p a o", p=P))
        nc.sync.dma_start(bias[:], b.rearrange("(a p) t -> p (a t)", p=P))

        ident = held.tile([P, P], BF16)
        make_identity(nc, ident[:])

        zeros = held.tile([P, S], BF16)
        nc.vector.memset(zeros[:], 0.0)
        idle_bank = psum.tile([P, S], F32)
        for i in range(WARM_UP):
            nc.tensor.matmul(idle_bank[:], zeros[:, :P], zeros[:], start=True, stop=True)
        silu_of_zero = held.tile([P, 1], F32)
        nc.scalar.activation(silu_of_zero[:], zeros[:, 0:1], SILU)

        windows = [psum.tile([P, S], F32, name=f"window{a}") for a in range(M_BLOCKS)]
        for a in range(M_BLOCKS):
            nc.tensor.matmul(windows[a][:], ident[:], base_sb[:, a, :], start=True, stop=False)

        for a in range(M_BLOCKS):
            for e in range(E):
                nc.tensor.matmul(
                    windows[a][:].indirect(offsets[:, e * PIECE : (e + 1) * PIECE]),
                    w_sb[:, e, a * P : (a + 1) * P],
                    x_sb[:, e * Q : (e + 1) * Q],
                    start=False,
                    stop=(e == E - 1),
                )

        z_sb = held.tile([P, M_BLOCKS, S], BF16)
        for a in range(M_BLOCKS):
            for h in range(H):
                cols = slice(h * HALF, (h + 1) * HALF)
                nc.vector.tensor_copy(z_sb[:, a, cols], windows[a][:, cols])

        y = [psum.tile([P, S], F32, name=f"y{o}") for o in range(O_BLOCKS)]
        out_sb = held.tile([P, O_BLOCKS, S], F32)
        for h in range(H):
            cols = slice(h * HALF, (h + 1) * HALF)
            for a in range(M_BLOCKS):
                for o in range(O_BLOCKS):
                    nc.tensor.matmul(
                        y[o][:, cols],
                        w2_sb[:, a, o * P : (o + 1) * P],
                        z_sb[:, a, cols],
                        start=(a == 0),
                        stop=(a == M_BLOCKS - 1),
                    )
            for o in range(O_BLOCKS):
                nc.scalar.activation(out_sb[:, o, cols], y[o][:, cols], SILU, bias=bias[:, o : o + 1])
                nc.sync.dma_start(out[o * P : (o + 1) * P, cols], out_sb[:, o, cols])
